import numpy as np
import ml_dtypes


def mxq(x, axis, fmt="e4m3"):
    dtype, down = {"e4m3": (ml_dtypes.float8_e4m3fn, 7), "e5m2": (ml_dtypes.float8_e5m2, 14)}[fmt]
    v = np.moveaxis(np.asarray(x, np.float32).astype(ml_dtypes.bfloat16).astype(np.float64), axis, -1)
    blocks = v.reshape(v.shape[:-1] + (-1, 32))
    amax = np.abs(blocks).max(-1, keepdims=True)
    byte = np.maximum(np.where(amax > 0, np.frexp(amax)[1] - 1 + 127, 0) - down, 1)
    scale = np.exp2(byte - 127.0)
    codes = (blocks / scale).astype(np.float32).astype(dtype).astype(np.float64)
    return np.moveaxis((codes * scale).reshape(v.shape), -1, axis)


WIDE = False


def mx_kscale(k):
    if not WIDE:
        return np.ones(k)
    levels = np.array([10, -10, 5, -5, 0])
    if k % 512:
        return np.exp2(np.random.permutation(np.resize(levels, k // 32))).repeat(32)
    a = np.empty((k // 512, 16))
    for p in range(k // 512):
        a[p, :8] = np.random.permutation(np.resize(levels, 8))
        for g in range(8):
            far = levels[np.abs(levels - a[p, g]) >= 10]
            a[p, g + 8] = far[np.random.randint(len(far))]
    return np.exp2(a.ravel()).repeat(32)


def f64(x):
    return np.asarray(x).astype(np.float64)


def striped(idx):
    return np.tile(idx.reshape(-1, 16).T, (8, 1)).astype(np.uint16)


def unstriped(offs):
    return offs[:16].T.reshape(-1).astype(np.int64)


def striped8(idx):
    return np.concatenate([x.reshape(-1, 16).T for x in idx]).astype(np.uint16)


def runs(offs, k):
    lists = np.stack([offs[16 * r : 16 * r + 16].T.reshape(-1) for r in range(8)]).astype(np.int64)
    return lists[np.arange(k) % 512 // 64]


def pack_weight(w):
    k, n = w.shape
    w = f64(np.asarray(w, np.float32).astype(ml_dtypes.bfloat16)).reshape(k // 32, 32, n)
    amax = np.abs(w).max(1)
    byte = np.clip(np.where(amax > 0, np.frexp(amax)[1] - 1 + 127 - 7, 1), 1, 254)
    scaled = (w * np.exp2(127.0 - byte)[:, None, :]).reshape(k, n).astype(np.float32)
    words = np.ascontiguousarray(scaled.reshape(k // 512, 128, 4, n).transpose(0, 1, 3, 2)).astype(ml_dtypes.float8_e4m3fn).view(np.uint8)
    return words, np.ascontiguousarray(byte.astype(np.uint8).reshape(k // 512, 16, n))


def unpack_weight(words, scales):
    g, p, n, _ = words.shape
    vals = np.ascontiguousarray(words).view(ml_dtypes.float8_e4m3fn).astype(np.float64) * np.repeat(np.exp2(scales.astype(np.float64) - 127.0), 8, axis=1)[..., None]
    return vals.transpose(0, 1, 3, 2).reshape(g * 512, n)


K, T, S, N, H = 512, 2048, 512, 512, 512


def setup_inputs():
    n = np.random.standard_normal
    s = mx_kscale(K)[:, None]
    u = mx_kscale(H)
    packed_xT = pack_weight(n((K, T)) * s)
    return {
        "x_words": packed_xT[0],
        "x_scales": packed_xT[1],
        "w1": (n((K, H)) / np.sqrt(K) / s).astype(np.float32),
        "w2": (n((K, H)) / np.sqrt(K) / s).astype(np.float32),
        "gn": (np.random.uniform(0.5, 1.5, (H, 1)) * u[:, None]).astype(np.float32),
        "w3": (n((H, N)) / np.sqrt(H) / u[:, None]).astype(np.float32),
        "offs": striped(np.random.permutation(T)[:S]),
        "two": striped(np.random.permutation(T)[:S]),
        "n1": striped8(np.stack([np.random.permutation(S) for _ in range(8)])),
        "n2": striped8(np.stack([np.random.permutation(S) for _ in range(8)])),
        "n3": striped8(np.stack([np.random.permutation(S) for _ in range(8)])),
        "n4": striped8(np.stack([np.random.permutation(S) for _ in range(8)])),
        "n5": striped8(np.stack([np.random.permutation(S) for _ in range(8)])),
    }


def reference(x_words, x_scales, w1, w2, gn, w3, offs, two, n1, n2, n3, n4, n5):
    x_two = unpack_weight(x_words, x_scales)[:, unstriped(two)]
    d = mxq(f64(w2), 0, "e4m3").T @ x_two
    xq = unpack_weight(x_words, x_scales)[:, unstriped(offs)]
    y = mxq(f64(w1), 0, "e4m3").T @ xq
    z = f64(gn) * (d * (y[np.arange(H)[:, None], runs(n1, H)] - y) + 0.5 * ((d[np.arange(H)[:, None], runs(n3, H)]) * (y[np.arange(H)[:, None], runs(n2, H)] - y)))
    h = mxq(f64(w3), 0, "e4m3").T @ mxq(z, 0, "e4m3")
    return h * (h[np.arange(N)[:, None], runs(n4, N)] - (h[np.arange(N)[:, None], runs(n5, N)]))

@@ -1,0 +1,236 @@
+from contextlib import ExitStack
+
+import concourse.mybir as mybir
+
+K, T, S, N, H = 512, 2048, 512, 512, 512
+FLOPS = 3 * 2 * 512 * 512 * 512
+
+F32 = mybir.dt.float32
+BF16 = mybir.dt.bfloat16
+I32 = mybir.dt.int32
+U32 = mybir.dt.uint32
+U16 = mybir.dt.uint16
+U8 = mybir.dt.uint8
+FP8X4 = mybir.dt.float8_e4m3fn_x4
+ALU = mybir.AluOpType
+COPY = mybir.ActivationFunctionType.Copy
+
+P = 128
+PACK = 4
+HALF = S // 2
+W1_VECTOR_SHARE = 72
+
+
+def tile_picked_twlflowbwind_none_p_kernel(
+    tc, x_words, x_scales, w1, w2, gn, w3, offs, two, n1, n2, n3, n4, n5, out
+):
+    nc = tc.nc
+    with ExitStack() as ctx:
+        keep = ctx.enter_context(tc.tile_pool(name="keep", bufs=1))
+        psum = ctx.enter_context(tc.psum_pool(name="psum", bufs=1))
+
+        def list_tile(name):
+            return keep.tile([P, S // 16], U16, name=name)
+
+        def load_list(tile, source):
+            nc.sync.dma_start(tile[:], source)
+
+        def part(tile, h):
+            return tile[:, h * HALF // 16 : (h + 1) * HALF // 16]
+
+        def cols(h):
+            return slice(h * HALF, (h + 1) * HALF)
+
+        l_offs, l_two, l1, l2, l3, l4, l5 = [list_tile(s) for s in ("l_offs", "l_two", "l1", "l2", "l3", "l4", "l5")]
+
+        xw = keep.tile([P, T], U32, name="xw", align_bytes=64)
+        xs = keep.tile([P, T], U8, name="xs", align_bytes=64)
+        raw = [keep.tile([P, PACK, H], F32, name="raw%d" % i) for i in range(3)]
+        gain = keep.tile([P, PACK], F32, name="gain")
+        half_gain = keep.tile([P, PACK], F32, name="half_gain")
+
+        def load_weight(i, w):
+            nc.sync.dma_start(out=raw[i][:], in_=w.rearrange("(p j) n -> p j n", j=PACK))
+
+        for q in range(4):
+            nc.sync.dma_start(
+                out=xs[32 * q : 32 * q + 32, :].bitcast(I32),
+                in_=x_scales[0, 4 * q : 4 * q + 4, :].bitcast(I32).unsqueeze(0).to_broadcast([8, 4, T // 4]),
+            )
+        load_list(l_offs, offs)
+        load_list(l_two, two)
+        load_weight(0, w1)
+        nc.sync.dma_start(out=xw[:].bitcast(I32), in_=x_words[0].rearrange("p n t -> p (n t)").bitcast(I32))
+        nc.sync.dma_start(out=gain[:], in_=gn.rearrange("(p t) o -> p (t o)", t=PACK))
+        load_list(l1, n1)
+        load_list(l2, n2)
+        load_weight(1, w2)
+        load_list(l3, n3)
+        load_weight(2, w3)
+        load_list(l4, n4)
+        load_list(l5, n5)
+
+        picked_w = [keep.tile([P, S], U32, name="picked_w%d" % i, align_bytes=64) for i in range(2)]
+        picked_s = [keep.tile([P, S], U8, name="picked_s%d" % i, align_bytes=64) for i in range(2)]
+        nc.vector.tensor_copy(out=picked_s[0][:], in_=xs[:].indirect(l_offs[:]))
+        nc.vector.tensor_copy(out=picked_s[1][:], in_=xs[:].indirect(l_two[:]))
+
+        grouped = [keep.tile([P, PACK * H], BF16, name="grouped%d" % i, align_bytes=64) for i in range(3)]
+        w_codes = [keep.tile([P, H], U32, name="w_codes%d" % i, align_bytes=64) for i in range(3)]
+        w_scales = [keep.tile([P, H], U8, name="w_scales%d" % i, align_bytes=64) for i in range(3)]
+
+        def group_views(i, m0, m1):
+            dst = grouped[i][:].rearrange("p (t m j) -> p m j t", t=PACK, j=PACK)[:, m0:m1]
+            src = raw[i][:].rearrange("p j (m t) -> p m j t", t=PACK)[:, m0:m1]
+            return dst, src
+
+        def group_on_vector(i, m0, m1):
+            dst, src = group_views(i, m0, m1)
+            nc.vector.tensor_copy(out=dst, in_=src)
+
+        def group_on_scalar(i, m0, m1):
+            dst, src = group_views(i, m0, m1)
+            nc.scalar.activation(out=dst, in_=src, func=COPY)
+
+        def quantize_weight(i, c0, c1):
+            nc.vector.quantize_mx(
+                out=w_codes[i][:, c0:c1].bitcast(FP8X4),
+                scales=w_scales[i][:, c0:c1],
+                in_=grouped[i][:, PACK * c0 : PACK * c1],
+            )
+
+        def product(acc, i, t, codes, scales):
+            nc.tensor.matmul_mx(
+                out=acc,
+                lhsT=w_codes[i][:, t * P : (t + 1) * P].bitcast(FP8X4),
+                lhsT_scale=w_scales[i][:, t * P : (t + 1) * P],
+                rhs=codes.bitcast(FP8X4),
+                rhs_scale=scales,
+                start=True,
+                stop=True,
+            )
+
+        group_on_scalar(0, W1_VECTOR_SHARE, P)
+        group_on_vector(0, 0, W1_VECTOR_SHARE)
+        quantize_weight(0, 0, H // 2)
+        quantize_weight(0, H // 2, H)
+        nc.vector.tensor_copy(out=picked_w[0][:], in_=xw[:].indirect(l_offs[:]))
+        nc.vector.tensor_copy(out=picked_w[1][:], in_=xw[:].indirect(l_two[:]))
+        y_acc = [psum.tile([P, S], F32, name="y_acc%d" % t, tag="bank%d" % t) for t in range(PACK)]
+        for t in range(PACK):
+            product(y_acc[t][:], 0, t, picked_w[0][:], picked_s[0][:])
+
+        nc.vector.tensor_scalar(out=half_gain[:], in0=gain[:], scalar1=0.5, scalar2=None, op0=ALU.mult)
+        group_on_vector(1, 0, P)
+        quantize_weight(1, 0, H // 2)
+        quantize_weight(1, H // 2, H)
+        d_acc = [psum.tile([P, S], F32, name="d_acc%d" % t, tag="bank%d" % (PACK + t)) for t in range(PACK)]
+        for t in range(PACK):
+            product(d_acc[t][:], 1, t, picked_w[1][:], picked_s[1][:])
+
+        y = [keep.tile([P, S], F32, name="y%d" % t) for t in range(PACK)]
+        e = [keep.tile([P, S], F32, name="e%d" % t) for t in range(PACK)]
+        fetched = [[keep.tile([P, 2, HALF], F32, name="fetched%d_%d" % (h, t)) for t in range(PACK)] for h in range(2)]
+        diffs = [[keep.tile([P, 2, HALF], F32, name="diffs%d_%d" % (h, t)) for t in range(PACK)] for h in range(2)]
+        near = [keep.tile([P, PACK, HALF], F32, name="near%d" % h) for h in range(2)]
+        far = [keep.tile([P, PACK, HALF], F32, name="far%d" % h) for h in range(2)]
+        z = [keep.tile([P, PACK * HALF], BF16, name="z%d" % h, align_bytes=64) for h in range(2)]
+        z_codes = [keep.tile([P, HALF], U32, name="z_codes%d" % h, align_bytes=64) for h in range(2)]
+        z_scales = [keep.tile([P, HALF], U8, name="z_scales%d" % h, align_bytes=64) for h in range(2)]
+
+        def fetch_y(h, t):
+            nc.scalar.activation(out=fetched[h][t][:, 0, :], in_=y[t][:].indirect(part(l1, h)), func=COPY)
+            nc.scalar.activation(out=fetched[h][t][:, 1, :], in_=y[t][:].indirect(part(l2, h)), func=COPY)
+
+        def subtract_y(h, t):
+            nc.vector.tensor_tensor(
+                out=diffs[h][t][:],
+                in0=fetched[h][t][:],
+                in1=y[t][:, cols(h)].unsqueeze(1).to_broadcast([P, 2, HALF]),
+                op=ALU.subtract,
+            )
+
+        def multiply(h, t):
+            nc.vector.tensor_tensor(
+                out=far[h][:, t, :], in0=e[t][:].indirect(part(l3, h)), in1=diffs[h][t][:, 1, :], op=ALU.mult
+            )
+            nc.vector.scalar_tensor_tensor(
+                out=near[h][:, t, :], in0=diffs[h][t][:, 0, :], scalar=2.0, in1=e[t][:, cols(h)], op0=ALU.mult, op1=ALU.mult
+            )
+
+        def finish_z(h):
+            nc.vector.tensor_tensor(
+                out=z[h][:].rearrange("p (c i t) -> p c t i", i=4, t=PACK),
+                in0=near[h][:].rearrange("p t (c i) -> p c t i", i=4),
+                in1=far[h][:].rearrange("p t (c i) -> p c t i", i=4),
+                op=ALU.add,
+            )
+
+        def quantize_z(h):
+            nc.vector.quantize_mx(out=z_codes[h][:].bitcast(FP8X4), scales=z_scales[h][:], in_=z[h][:])
+
+        def evacuate_d(t):
+            nc.scalar.activation(out=e[t][:], in_=d_acc[t][:], func=COPY, scale=half_gain[:, t : t + 1])
+
+        for t in range(PACK):
+            nc.scalar.activation(out=y[t][:], in_=y_acc[t][:], func=COPY)
+            fetch_y(0, t)
+            subtract_y(0, t)
+            if t > 0:
+                evacuate_d(t - 1)
+                multiply(0, t - 1)
+        evacuate_d(PACK - 1)
+        fetch_y(1, 0)
+        multiply(0, PACK - 1)
+        subtract_y(1, 0)
+        finish_z(0)
+        for t in range(1, PACK):
+            fetch_y(1, t)
+            multiply(1, t - 1)
+            if t == 1:
+                quantize_z(0)
+            subtract_y(1, t)
+        group_on_scalar(2, 0, P // 2)
+        group_on_scalar(2, P // 2, P)
+        multiply(1, PACK - 1)
+        quantize_weight(2, 0, H)
+        finish_z(1)
+
+        h_acc = [[psum.tile([P, HALF], F32, name="h_acc%d_%d" % (h, t), tag="bank%d" % (PACK * h + t)) for t in range(PACK)] for h in range(2)]
+        hh = [keep.tile([P, S], F32, name="hh%d" % t) for t in range(PACK)]
+        for t in range(PACK):
+            product(h_acc[0][t][:], 2, t, z_codes[0][:], z_scales[0][:])
+            nc.scalar.activation(out=hh[t][:, cols(0)], in_=h_acc[0][t][:], func=COPY)
+        quantize_z(1)
+        for t in range(PACK):
+            product(h_acc[1][t][:], 2, t, z_codes[1][:], z_scales[1][:])
+        nc.scalar.activation(out=hh[0][:, cols(1)], in_=h_acc[1][0][:], func=COPY)
+        nc.vector.tensor_copy(out=hh[1][:, cols(1)], in_=h_acc[1][1][:])
+        nc.vector.tensor_copy(out=hh[2][:, cols(1)], in_=h_acc[1][2][:])
+
+        out_rows = out.rearrange("(p t) j -> p t j", t=PACK)
+        at5 = [[keep.tile([P, HALF], F32, name="at5_%d_%d" % (h, t)) for t in range(PACK)] for h in range(2)]
+        at4 = [[keep.tile([P, HALF], F32, name="at4_%d_%d" % (h, t)) for t in range(PACK)] for h in range(2)]
+        gap = [[keep.tile([P, HALF], F32, name="gap%d_%d" % (h, t)) for t in range(PACK)] for h in range(2)]
+        res = [[keep.tile([P, HALF], F32, name="res%d_%d" % (h, t)) for t in range(PACK)] for h in range(2)]
+
+        def difference(h, t, both_on_scalar):
+            nc.scalar.activation(out=at5[h][t][:], in_=hh[t][:].indirect(part(l5, h)), func=COPY)
+            if both_on_scalar:
+                nc.scalar.activation(out=at4[h][t][:], in_=hh[t][:].indirect(part(l4, h)), func=COPY)
+                nc.vector.tensor_tensor(out=gap[h][t][:], in0=at4[h][t][:], in1=at5[h][t][:], op=ALU.subtract)
+            else:
+                nc.vector.tensor_tensor(out=gap[h][t][:], in0=hh[t][:].indirect(part(l4, h)), in1=at5[h][t][:], op=ALU.subtract)
+
+        def finish(h, t):
+            nc.vector.tensor_tensor(out=res[h][t][:], in0=gap[h][t][:], in1=hh[t][:, cols(h)], op=ALU.mult)
+            nc.sync.dma_start(out=out_rows[:, t, cols(h)], in_=res[h][t][:])
+
+        chunks = [(h, t) for t in range(PACK) for h in range(2)]
+        for i, (h, t) in enumerate(chunks):
+            if (h, t) == (0, 2):
+                nc.scalar.activation(out=hh[3][:, cols(1)], in_=h_acc[1][3][:], func=COPY)
+            difference(h, t, h == 1 and t in (1, 2))
+            if i > 0:
+                finish(*chunks[i - 1])
+        finish(*chunks[-1])

@@ -27,6 +27,7 @@ def tile_picked_twlflowbwind_none_p_kernel(
     nc = tc.nc
     with ExitStack() as ctx:
         keep = ctx.enter_context(tc.tile_pool(name="keep", bufs=1))
+        shared = ctx.enter_context(tc.tile_pool(name="shared", bufs=1))
         psum = ctx.enter_context(tc.psum_pool(name="psum", bufs=1))
 
         def list_tile(name):
@@ -45,7 +46,11 @@ def tile_picked_twlflowbwind_none_p_kernel(
 
         xw = keep.tile([P, T], U32, name="xw", align_bytes=64)
         xs = keep.tile([P, T], U8, name="xs", align_bytes=64)
-        raw = [keep.tile([P, PACK, H], F32, name="raw%d" % i) for i in range(3)]
+        raw = [
+            keep.tile([P, PACK, H], F32, name="raw0"),
+            shared.tile([P, PACK, H], F32, name="raw1", offset=0),
+            keep.tile([P, PACK, H], F32, name="raw2"),
+        ]
         gain = keep.tile([P, PACK], F32, name="gain")
         half_gain = keep.tile([P, PACK], F32, name="half_gain")
 
@@ -59,9 +64,9 @@ def tile_picked_twlflowbwind_none_p_kernel(
             )
         load_list(l_offs, offs)
         load_list(l_two, two)
-        load_weight(0, w1)
         nc.sync.dma_start(out=xw[:].bitcast(I32), in_=x_words[0].rearrange("p n t -> p (n t)").bitcast(I32))
         nc.sync.dma_start(out=gain[:], in_=gn.rearrange("(p t) o -> p (t o)", t=PACK))
+        load_weight(0, w1)
         load_list(l1, n1)
         load_list(l2, n2)
         load_weight(1, w2)
@@ -74,10 +79,15 @@ def tile_picked_twlflowbwind_none_p_kernel(
         picked_s = [keep.tile([P, S], U8, name="picked_s%d" % i, align_bytes=64) for i in range(2)]
         nc.vector.tensor_copy(out=picked_s[0][:], in_=xs[:].indirect(l_offs[:]))
         nc.vector.tensor_copy(out=picked_s[1][:], in_=xs[:].indirect(l_two[:]))
+        nc.vector.tensor_copy(out=picked_w[0][:], in_=xw[:].indirect(l_offs[:]))
+        nc.vector.tensor_copy(out=picked_w[1][:], in_=xw[:].indirect(l_two[:]))
 
-        grouped = [keep.tile([P, PACK * H], BF16, name="grouped%d" % i, align_bytes=64) for i in range(3)]
+        grouped = {}
         w_codes = [keep.tile([P, H], U32, name="w_codes%d" % i, align_bytes=64) for i in range(3)]
         w_scales = [keep.tile([P, H], U8, name="w_scales%d" % i, align_bytes=64) for i in range(3)]
+
+        def new_grouped(i, tag):
+            grouped[i] = keep.tile([P, PACK * H], BF16, name="grouped%d" % i, tag=tag, align_bytes=64)
 
         def group_views(i, m0, m1):
             dst = grouped[i][:].rearrange("p (t m j) -> p m j t", t=PACK, j=PACK)[:, m0:m1]
@@ -110,127 +120,207 @@ def tile_picked_twlflowbwind_none_p_kernel(
                 stop=True,
             )
 
+        nc.scalar.activation(out=half_gain[:], in_=gain[:], func=COPY, scale=0.5)
+        new_grouped(0, "grouped")
         group_on_scalar(0, W1_VECTOR_SHARE, P)
         group_on_vector(0, 0, W1_VECTOR_SHARE)
-        quantize_weight(0, 0, H // 2)
-        quantize_weight(0, H // 2, H)
-        nc.vector.tensor_copy(out=picked_w[0][:], in_=xw[:].indirect(l_offs[:]))
-        nc.vector.tensor_copy(out=picked_w[1][:], in_=xw[:].indirect(l_two[:]))
+        quantize_weight(0, 0, P)
+        quantize_weight(0, P, H)
         y_acc = [psum.tile([P, S], F32, name="y_acc%d" % t, tag="bank%d" % t) for t in range(PACK)]
         for t in range(PACK):
             product(y_acc[t][:], 0, t, picked_w[0][:], picked_s[0][:])
 
-        nc.vector.tensor_scalar(out=half_gain[:], in0=gain[:], scalar1=0.5, scalar2=None, op0=ALU.mult)
-        group_on_vector(1, 0, P)
-        quantize_weight(1, 0, H // 2)
-        quantize_weight(1, H // 2, H)
-        d_acc = [psum.tile([P, S], F32, name="d_acc%d" % t, tag="bank%d" % (PACK + t)) for t in range(PACK)]
-        for t in range(PACK):
-            product(d_acc[t][:], 1, t, picked_w[1][:], picked_s[1][:])
-
-        y = [keep.tile([P, S], F32, name="y%d" % t) for t in range(PACK)]
-        e = [keep.tile([P, S], F32, name="e%d" % t) for t in range(PACK)]
-        fetched = [[keep.tile([P, 2, HALF], F32, name="fetched%d_%d" % (h, t)) for t in range(PACK)] for h in range(2)]
-        diffs = [[keep.tile([P, 2, HALF], F32, name="diffs%d_%d" % (h, t)) for t in range(PACK)] for h in range(2)]
-        near = [keep.tile([P, PACK, HALF], F32, name="near%d" % h) for h in range(2)]
-        far = [keep.tile([P, PACK, HALF], F32, name="far%d" % h) for h in range(2)]
+        whole = slice(0, S)
+        last = PACK - 1
+        fetched = {}
+        diffs = {}
+        near = keep.tile([P, PACK, S], F32, name="near")
+        far = keep.tile([P, PACK, S], F32, name="far")
         z = [keep.tile([P, PACK * HALF], BF16, name="z%d" % h, align_bytes=64) for h in range(2)]
         z_codes = [keep.tile([P, HALF], U32, name="z_codes%d" % h, align_bytes=64) for h in range(2)]
         z_scales = [keep.tile([P, HALF], U8, name="z_scales%d" % h, align_bytes=64) for h in range(2)]
 
-        def fetch_y(h, t):
-            nc.scalar.activation(out=fetched[h][t][:, 0, :], in_=y[t][:].indirect(part(l1, h)), func=COPY)
-            nc.scalar.activation(out=fetched[h][t][:, 1, :], in_=y[t][:].indirect(part(l2, h)), func=COPY)
+        def entries(tile, c):
+            return tile[:, c.start // 16 : c.stop // 16]
 
-        def subtract_y(h, t):
+        def fetch(t, c, slot, with_e=False):
+            n = c.stop - c.start
+            fetched[t, c.start] = keep.tile([P, 3 if with_e else 2, n], F32, name="fetched%d_%d" % (t, c.start), tag=slot)
+            for i, offsets in enumerate((l1, l2)):
+                for c0 in range(0, n, HALF):
+                    nc.scalar.activation(
+                        out=fetched[t, c.start][:, i, c0 : c0 + HALF],
+                        in_=y[t][:].indirect(entries(offsets, slice(c.start + c0, c.start + c0 + HALF))),
+                        func=COPY,
+                    )
+            if with_e:
+                nc.scalar.activation(out=fetched[t, c.start][:, 2, :], in_=e[t][:].indirect(entries(l3, c)), func=COPY)
+
+        def subtract_y(t, c):
             nc.vector.tensor_tensor(
-                out=diffs[h][t][:],
-                in0=fetched[h][t][:],
-                in1=y[t][:, cols(h)].unsqueeze(1).to_broadcast([P, 2, HALF]),
+                out=diffs[t][:, :, c],
+                in0=fetched[t, c.start][:, 0:2, :],
+                in1=y[t][:, c].unsqueeze(1).to_broadcast([P, 2, c.stop - c.start]),
                 op=ALU.subtract,
             )
 
-        def multiply(h, t):
-            nc.vector.tensor_tensor(
-                out=far[h][:, t, :], in0=e[t][:].indirect(part(l3, h)), in1=diffs[h][t][:, 1, :], op=ALU.mult
-            )
+        def near_term(t, c):
             nc.vector.scalar_tensor_tensor(
-                out=near[h][:, t, :], in0=diffs[h][t][:, 0, :], scalar=2.0, in1=e[t][:, cols(h)], op0=ALU.mult, op1=ALU.mult
+                out=near[:, t, c], in0=diffs[t][:, 0, c], scalar=2.0, in1=e[t][:, c], op0=ALU.mult, op1=ALU.mult
             )
 
-        def finish_z(h):
+        def far_term(t, c):
+            for c0 in range(c.start, c.stop, HALF):
+                nc.vector.tensor_tensor(
+                    out=far[:, t, c0 : c0 + HALF],
+                    in0=e[t][:].indirect(entries(l3, slice(c0, c0 + HALF))),
+                    in1=diffs[t][:, 1, c0 : c0 + HALF],
+                    op=ALU.mult,
+                )
+
+        def far_term_fetched(t, c):
+            nc.vector.tensor_tensor(
+                out=far[:, t, c], in0=fetched[t, c.start][:, 2, :], in1=diffs[t][:, 1, c], op=ALU.mult
+            )
+
+        def add_terms(h):
             nc.vector.tensor_tensor(
                 out=z[h][:].rearrange("p (c i t) -> p c t i", i=4, t=PACK),
-                in0=near[h][:].rearrange("p t (c i) -> p c t i", i=4),
-                in1=far[h][:].rearrange("p t (c i) -> p c t i", i=4),
+                in0=near[:, :, cols(h)].rearrange("p t (c i) -> p c t i", i=4),
+                in1=far[:, :, cols(h)].rearrange("p t (c i) -> p c t i", i=4),
                 op=ALU.add,
             )
 
         def quantize_z(h):
             nc.vector.quantize_mx(out=z_codes[h][:].bitcast(FP8X4), scales=z_scales[h][:], in_=z[h][:])
 
-        def evacuate_d(t):
-            nc.scalar.activation(out=e[t][:], in_=d_acc[t][:], func=COPY, scale=half_gain[:, t : t + 1])
+        y = {0: keep.tile([P, S], F32, name="y0")}
+        e = [keep.tile([P, S], F32, name="e%d" % t) for t in range(PACK)]
 
+        def y_on_scalar(t):
+            nc.scalar.activation(out=y[t][:, whole], in_=y_acc[t][:], func=COPY)
+
+        def d_on_scalar(t):
+            nc.scalar.activation(out=e[t][:, whole], in_=d_acc[t][:], func=COPY, scale=half_gain[:, t : t + 1])
+
+        def y_on_vector(t):
+            nc.vector.tensor_copy(out=y[t][:, whole], in_=y_acc[t][:])
+
+        first, second = cols(0), cols(1)
+        y_on_scalar(0)
+        fetch(0, first, "slot_a")
+        fetch(0, second, "slot_b")
+        new_grouped(1, "grouped")
+        group_on_vector(1, 0, P)
+        y[1] = shared.tile([P, S], F32, name="y1", offset=2 * S * 4)
+        y[2] = shared.tile([P, S], F32, name="y2", offset=0)
+        y_on_vector(1)
+        quantize_weight(1, 0, P)
+        quantize_weight(1, P, H)
+        d_acc = [psum.tile([P, S], F32, name="d_acc%d" % t, tag="bank%d" % (PACK + t)) for t in range(PACK)]
         for t in range(PACK):
-            nc.scalar.activation(out=y[t][:], in_=y_acc[t][:], func=COPY)
-            fetch_y(0, t)
-            subtract_y(0, t)
-            if t > 0:
-                evacuate_d(t - 1)
-                multiply(0, t - 1)
-        evacuate_d(PACK - 1)
-        fetch_y(1, 0)
-        multiply(0, PACK - 1)
-        subtract_y(1, 0)
-        finish_z(0)
+            product(d_acc[t][:], 1, t, picked_w[1][:], picked_s[1][:])
+        diffs[0] = keep.tile([P, 2, S], F32, name="diffs0", tag="grouped", align_bytes=64)
         for t in range(1, PACK):
-            fetch_y(1, t)
-            multiply(1, t - 1)
-            if t == 1:
-                quantize_z(0)
-            subtract_y(1, t)
-        group_on_scalar(2, 0, P // 2)
-        group_on_scalar(2, P // 2, P)
-        multiply(1, PACK - 1)
+            diffs[t] = keep.tile([P, 2, S], F32, name="diffs%d" % t)
+        fetch(1, first, "slot_c")
+        fetch(1, second, "slot_d")
+        y_on_vector(2)
+        nc.vector.tensor_scalar(out=e[0][:, whole], in0=d_acc[0][:], scalar1=half_gain[:, 0:1], scalar2=None, op0=ALU.mult)
+        subtract_y(0, first)
+        subtract_y(0, second)
+        near_term(0, first)
+        far_term(0, first)
+        far_term(0, second)
+        near_term(0, second)
+        d_on_scalar(1)
+        fetch(2, first, "slot_b")
+        subtract_y(1, first)
+        subtract_y(1, second)
+        near_term(1, first)
+        far_term(1, first)
+        far_term(1, second)
+        y[3] = keep.tile([P, S], F32, name="y3", tag="slot_a")
+        y_on_scalar(3)
+        d_on_scalar(2)
+        fetch(3, first, "slot_c")
+        d_on_scalar(3)
+        subtract_y(2, first)
+        near_term(1, second)
+        far_term(2, first)
+        subtract_y(3, first)
+        near_term(2, first)
+        grouped[2] = shared.tile([P, PACK * H], BF16, name="grouped2", offset=2 * S * 4, align_bytes=64)
+        group_on_scalar(2, 0, P)
+        fetch(2, second, "slot_b")
+        far_term(3, first)
+        near_term(3, first)
         quantize_weight(2, 0, H)
-        finish_z(1)
-
+        add_terms(0)
+        subtract_y(2, second)
+        quantize_z(0)
         h_acc = [[psum.tile([P, HALF], F32, name="h_acc%d_%d" % (h, t), tag="bank%d" % (PACK * h + t)) for t in range(PACK)] for h in range(2)]
-        hh = [keep.tile([P, S], F32, name="hh%d" % t) for t in range(PACK)]
         for t in range(PACK):
             product(h_acc[0][t][:], 2, t, z_codes[0][:], z_scales[0][:])
-            nc.scalar.activation(out=hh[t][:, cols(0)], in_=h_acc[0][t][:], func=COPY)
+        fetch(3, second, "slot_c", True)
+        far_term(2, second)
+        subtract_y(last, second)
+        near_term(2, second)
+        near_term(last, second)
+        far_term_fetched(last, second)
+        add_terms(1)
+        wide = [diffs[t][:].rearrange("p a n -> p (a n)") for t in range(2)]
+        hh = [y[0][:], wide[0], wide[1], e[0][:]]
+        for t in range(PACK):
+            nc.scalar.activation(out=hh[t][:, first], in_=h_acc[0][t][:], func=COPY)
         quantize_z(1)
         for t in range(PACK):
             product(h_acc[1][t][:], 2, t, z_codes[1][:], z_scales[1][:])
-        nc.scalar.activation(out=hh[0][:, cols(1)], in_=h_acc[1][0][:], func=COPY)
-        nc.vector.tensor_copy(out=hh[1][:, cols(1)], in_=h_acc[1][1][:])
-        nc.vector.tensor_copy(out=hh[2][:, cols(1)], in_=h_acc[1][2][:])
+        nc.scalar.activation(out=hh[0][:, second], in_=h_acc[1][0][:], func=COPY)
+        for t in range(1, PACK):
+            nc.vector.tensor_copy(out=hh[t][:, second], in_=h_acc[1][t][:])
 
         out_rows = out.rearrange("(p t) j -> p t j", t=PACK)
-        at5 = [[keep.tile([P, HALF], F32, name="at5_%d_%d" % (h, t)) for t in range(PACK)] for h in range(2)]
-        at4 = [[keep.tile([P, HALF], F32, name="at4_%d_%d" % (h, t)) for t in range(PACK)] for h in range(2)]
-        gap = [[keep.tile([P, HALF], F32, name="gap%d_%d" % (h, t)) for t in range(PACK)] for h in range(2)]
-        res = [[keep.tile([P, HALF], F32, name="res%d_%d" % (h, t)) for t in range(PACK)] for h in range(2)]
+        at5 = [keep.tile([P, S], F32, name="at5_%d" % t) for t in range(PACK)]
+        at4 = keep.tile([P, S], F32, name="at4")
+        gap = {}
 
-        def difference(h, t, both_on_scalar):
-            nc.scalar.activation(out=at5[h][t][:], in_=hh[t][:].indirect(part(l5, h)), func=COPY)
-            if both_on_scalar:
-                nc.scalar.activation(out=at4[h][t][:], in_=hh[t][:].indirect(part(l4, h)), func=COPY)
-                nc.vector.tensor_tensor(out=gap[h][t][:], in0=at4[h][t][:], in1=at5[h][t][:], op=ALU.subtract)
-            else:
-                nc.vector.tensor_tensor(out=gap[h][t][:], in0=hh[t][:].indirect(part(l4, h)), in1=at5[h][t][:], op=ALU.subtract)
+        def new_gap(t, c, slot):
+            gap[t, c.start] = keep.tile([P, c.stop - c.start], F32, name="gap%d_%d" % (t, c.start), tag=slot)
 
-        def finish(h, t):
-            nc.vector.tensor_tensor(out=res[h][t][:], in0=gap[h][t][:], in1=hh[t][:, cols(h)], op=ALU.mult)
-            nc.sync.dma_start(out=out_rows[:, t, cols(h)], in_=res[h][t][:])
+        res = [keep.tile([P, S], F32, name="res%d" % t) for t in range(PACK)]
 
-        chunks = [(h, t) for t in range(PACK) for h in range(2)]
-        for i, (h, t) in enumerate(chunks):
-            if (h, t) == (0, 2):
-                nc.scalar.activation(out=hh[3][:, cols(1)], in_=h_acc[1][3][:], func=COPY)
-            difference(h, t, h == 1 and t in (1, 2))
-            if i > 0:
-                finish(*chunks[i - 1])
-        finish(*chunks[-1])
+        def fetch5(t, c):
+            nc.scalar.activation(out=at5[t][:, c], in_=hh[t].indirect(entries(l5, c)), func=COPY)
+
+        def fused_gap(t, c, slot):
+            new_gap(t, c, slot)
+            nc.vector.tensor_tensor(out=gap[t, c.start][:], in0=hh[t].indirect(entries(l4, c)), in1=at5[t][:, c], op=ALU.subtract)
+
+        def plain_gap(t, c, slot):
+            new_gap(t, c, slot)
+            nc.scalar.activation(out=at4[:, c], in_=hh[t].indirect(entries(l4, c)), func=COPY)
+            nc.vector.tensor_tensor(out=gap[t, c.start][:], in0=at4[:, c], in1=at5[t][:, c], op=ALU.subtract)
+
+        def finish(t, c):
+            nc.vector.tensor_tensor(out=res[t][:, c], in0=gap[t, c.start][:], in1=hh[t][:, c], op=ALU.mult)
+            nc.sync.dma_start(out=out_rows[:, t, c], in_=res[t][:, c])
+
+        fetch5(0, first)
+        fused_gap(0, first, "gap_a")
+        fetch5(0, second)
+        fused_gap(0, second, "gap_b")
+        fetch5(1, whole)
+        finish(0, first)
+        finish(0, second)
+        fused_gap(1, whole, "gap_a")
+        fetch5(2, whole)
+        fused_gap(2, whole, "gap_b")
+        finish(1, whole)
+        finish(2, whole)
+        fetch5(last, first)
+        plain_gap(last, first, "gap_a")
+        fetch5(last, second)
+        plain_gap(last, second, "gap_b")
+        finish(last, first)
+        finish(last, second)

@@ -64,9 +64,9 @@ def tile_picked_twlflowbwind_none_p_kernel(
             )
         load_list(l_offs, offs)
         load_list(l_two, two)
+        load_weight(0, w1)
         nc.sync.dma_start(out=xw[:].bitcast(I32), in_=x_words[0].rearrange("p n t -> p (n t)").bitcast(I32))
         nc.sync.dma_start(out=gain[:], in_=gn.rearrange("(p t) o -> p (t o)", t=PACK))
-        load_weight(0, w1)
         load_list(l1, n1)
         load_list(l2, n2)
         load_weight(1, w2)
@@ -79,8 +79,6 @@ def tile_picked_twlflowbwind_none_p_kernel(
         picked_s = [keep.tile([P, S], U8, name="picked_s%d" % i, align_bytes=64) for i in range(2)]
         nc.vector.tensor_copy(out=picked_s[0][:], in_=xs[:].indirect(l_offs[:]))
         nc.vector.tensor_copy(out=picked_s[1][:], in_=xs[:].indirect(l_two[:]))
-        nc.vector.tensor_copy(out=picked_w[0][:], in_=xw[:].indirect(l_offs[:]))
-        nc.vector.tensor_copy(out=picked_w[1][:], in_=xw[:].indirect(l_two[:]))
 
         grouped = {}
         w_codes = [keep.tile([P, H], U32, name="w_codes%d" % i, align_bytes=64) for i in range(3)]
@@ -98,9 +96,10 @@ def tile_picked_twlflowbwind_none_p_kernel(
             dst, src = group_views(i, m0, m1)
             nc.vector.tensor_copy(out=dst, in_=src)
 
-        def group_on_scalar(i, m0, m1):
-            dst, src = group_views(i, m0, m1)
-            nc.scalar.activation(out=dst, in_=src, func=COPY)
+        def group_on_gpsimd(i, t):
+            dst = grouped[i][:].rearrange("p (t a b j) -> p t a b j", t=PACK, b=8, j=PACK)[:, t]
+            src = raw[i][:].rearrange("p j (a t b) -> p t a b j", t=PACK, b=8)[:, t]
+            nc.gpsimd.tensor_copy(out=dst, in_=src)
 
         def quantize_weight(i, c0, c1):
             nc.vector.quantize_mx(
@@ -122,10 +121,10 @@ def tile_picked_twlflowbwind_none_p_kernel(
 
         nc.scalar.activation(out=half_gain[:], in_=gain[:], func=COPY, scale=0.5)
         new_grouped(0, "grouped")
-        group_on_scalar(0, W1_VECTOR_SHARE, P)
-        group_on_vector(0, 0, W1_VECTOR_SHARE)
-        quantize_weight(0, 0, P)
-        quantize_weight(0, P, H)
+        group_on_vector(0, 0, P)
+        quantize_weight(0, 0, H)
+        nc.vector.tensor_copy(out=picked_w[0][:], in_=xw[:].indirect(l_offs[:]))
+        nc.vector.tensor_copy(out=picked_w[1][:], in_=xw[:].indirect(l_two[:]))
         y_acc = [psum.tile([P, S], F32, name="y_acc%d" % t, tag="bank%d" % t) for t in range(PACK)]
         for t in range(PACK):
             product(y_acc[t][:], 0, t, picked_w[0][:], picked_s[0][:])
@@ -160,13 +159,13 @@ def tile_picked_twlflowbwind_none_p_kernel(
             nc.vector.tensor_tensor(
                 out=diffs[t][:, :, c],
                 in0=fetched[t, c.start][:, 0:2, :],
-                in1=y[t][:, c].unsqueeze(1).to_broadcast([P, 2, c.stop - c.start]),
+                in1=y_acc[t][:, c].unsqueeze(1).to_broadcast([P, 2, c.stop - c.start]),
                 op=ALU.subtract,
             )
 
         def near_term(t, c):
             nc.vector.scalar_tensor_tensor(
-                out=near[:, t, c], in0=diffs[t][:, 0, c], scalar=2.0, in1=e[t][:, c], op0=ALU.mult, op1=ALU.mult
+                out=near[:, t, c], in0=diffs[t][:, 0, c], scalar=gain[:, t : t + 1], in1=d_acc[t][:, c], op0=ALU.mult, op1=ALU.mult
             )
 
         def far_term(t, c):
@@ -225,17 +224,20 @@ def tile_picked_twlflowbwind_none_p_kernel(
             diffs[t] = keep.tile([P, 2, S], F32, name="diffs%d" % t)
         fetch(1, first, "slot_c")
         fetch(1, second, "slot_d")
+        grouped[2] = keep.tile([P, PACK * H], BF16, name="grouped2", align_bytes=64)
+        for t in range(PACK):
+            group_on_gpsimd(2, t)
         y_on_vector(2)
         nc.vector.tensor_scalar(out=e[0][:, whole], in0=d_acc[0][:], scalar1=half_gain[:, 0:1], scalar2=None, op0=ALU.mult)
         subtract_y(0, first)
         subtract_y(0, second)
         near_term(0, first)
+        near_term(0, second)
+        subtract_y(1, first)
         far_term(0, first)
         far_term(0, second)
-        near_term(0, second)
         d_on_scalar(1)
         fetch(2, first, "slot_b")
-        subtract_y(1, first)
         subtract_y(1, second)
         near_term(1, first)
         far_term(1, first)
@@ -243,27 +245,26 @@ def tile_picked_twlflowbwind_none_p_kernel(
         y[3] = keep.tile([P, S], F32, name="y3", tag="slot_a")
         y_on_scalar(3)
         d_on_scalar(2)
-        fetch(3, first, "slot_c")
         d_on_scalar(3)
+        fetch(3, first, "slot_c", True)
         subtract_y(2, first)
         near_term(1, second)
         far_term(2, first)
         subtract_y(3, first)
         near_term(2, first)
-        grouped[2] = shared.tile([P, PACK * H], BF16, name="grouped2", offset=2 * S * 4, align_bytes=64)
-        group_on_scalar(2, 0, P)
-        fetch(2, second, "slot_b")
-        far_term(3, first)
+        fetch(2, second, "slot_b", True)
+        far_term_fetched(3, first)
         near_term(3, first)
         quantize_weight(2, 0, H)
         add_terms(0)
         subtract_y(2, second)
         quantize_z(0)
-        h_acc = [[psum.tile([P, HALF], F32, name="h_acc%d_%d" % (h, t), tag="bank%d" % (PACK * h + t)) for t in range(PACK)] for h in range(2)]
+        h_banks = ((0, 1, PACK, PACK + 1), (2, 3, PACK + 2, PACK + 3))
+        h_acc = [[psum.tile([P, HALF], F32, name="h_acc0_%d" % t, tag="bank%d" % h_banks[0][t]) for t in range(PACK)]]
         for t in range(PACK):
             product(h_acc[0][t][:], 2, t, z_codes[0][:], z_scales[0][:])
         fetch(3, second, "slot_c", True)
-        far_term(2, second)
+        far_term_fetched(2, second)
         subtract_y(last, second)
         near_term(2, second)
         near_term(last, second)
@@ -274,13 +275,14 @@ def tile_picked_twlflowbwind_none_p_kernel(
         for t in range(PACK):
             nc.scalar.activation(out=hh[t][:, first], in_=h_acc[0][t][:], func=COPY)
         quantize_z(1)
+        h_acc.append([psum.tile([P, HALF], F32, name="h_acc1_%d" % t, tag="bank%d" % h_banks[1][t]) for t in range(PACK)])
         for t in range(PACK):
             product(h_acc[1][t][:], 2, t, z_codes[1][:], z_scales[1][:])
         nc.scalar.activation(out=hh[0][:, second], in_=h_acc[1][0][:], func=COPY)
         for t in range(1, PACK):
             nc.vector.tensor_copy(out=hh[t][:, second], in_=h_acc[1][t][:])
 
-        out_rows = out.rearrange("(p t) j -> p t j", t=PACK)
+        out_rows = out.rearrange("(a t b) j -> t a b j", t=PACK, b=8)
         at5 = [keep.tile([P, S], F32, name="at5_%d" % t) for t in range(PACK)]
         at4 = keep.tile([P, S], F32, name="at4")
         gap = {}
@@ -304,7 +306,7 @@ def tile_picked_twlflowbwind_none_p_kernel(
 
         def finish(t, c):
             nc.vector.tensor_tensor(out=res[t][:, c], in0=gap[t, c.start][:], in1=hh[t][:, c], op=ALU.mult)
-            nc.sync.dma_start(out=out_rows[:, t, c], in_=res[t][:, c])
+            nc.sync.dma_start(out=out_rows[t][:, :, c], in_=res[t][:, c])
 
         fetch5(0, first)
         fused_gap(0, first, "gap_a")

from contextlib import ExitStack

import concourse.mybir as mybir

K, T, S, N, H = 512, 2048, 512, 512, 512
FLOPS = 3 * 2 * 512 * 512 * 512

F32 = mybir.dt.float32
BF16 = mybir.dt.bfloat16
I32 = mybir.dt.int32
U32 = mybir.dt.uint32
U16 = mybir.dt.uint16
U8 = mybir.dt.uint8
FP8X4 = mybir.dt.float8_e4m3fn_x4
ALU = mybir.AluOpType
COPY = mybir.ActivationFunctionType.Copy

P = 128
PACK = 4
HALF = S // 2
W1_VECTOR_SHARE = 72


def tile_picked_twlflowbwind_none_p_kernel(
    tc, x_words, x_scales, w1, w2, gn, w3, offs, two, n1, n2, n3, n4, n5, out
):
    nc = tc.nc
    with ExitStack() as ctx:
        keep = ctx.enter_context(tc.tile_pool(name="keep", bufs=1))
        shared = ctx.enter_context(tc.tile_pool(name="shared", bufs=1))
        psum = ctx.enter_context(tc.psum_pool(name="psum", bufs=1))

        def list_tile(name):
            return keep.tile([P, S // 16], U16, name=name)

        def load_list(tile, source):
            nc.sync.dma_start(tile[:], source)

        def part(tile, h):
            return tile[:, h * HALF // 16 : (h + 1) * HALF // 16]

        def cols(h):
            return slice(h * HALF, (h + 1) * HALF)

        l_offs, l_two, l1, l2, l3, l4, l5 = [list_tile(s) for s in ("l_offs", "l_two", "l1", "l2", "l3", "l4", "l5")]

        xw = keep.tile([P, T], U32, name="xw", align_bytes=64)
        xs = keep.tile([P, T], U8, name="xs", align_bytes=64)
        raw = [
            keep.tile([P, PACK, H], F32, name="raw0"),
            shared.tile([P, PACK, H], F32, name="raw1", offset=0),
            keep.tile([P, PACK, H], F32, name="raw2"),
        ]
        gain = keep.tile([P, PACK], F32, name="gain")
        half_gain = keep.tile([P, PACK], F32, name="half_gain")

        def load_weight(i, w):
            nc.sync.dma_start(out=raw[i][:], in_=w.rearrange("(p j) n -> p j n", j=PACK))

        for q in range(4):
            nc.sync.dma_start(
                out=xs[32 * q : 32 * q + 32, :].bitcast(I32),
                in_=x_scales[0, 4 * q : 4 * q + 4, :].bitcast(I32).unsqueeze(0).to_broadcast([8, 4, T // 4]),
            )
        load_list(l_offs, offs)
        load_list(l_two, two)
        load_weight(0, w1)
        nc.sync.dma_start(out=xw[:].bitcast(I32), in_=x_words[0].rearrange("p n t -> p (n t)").bitcast(I32))
        nc.sync.dma_start(out=gain[:], in_=gn.rearrange("(p t) o -> p (t o)", t=PACK))
        load_list(l1, n1)
        load_list(l2, n2)
        load_weight(1, w2)
        load_list(l3, n3)
        load_weight(2, w3)
        load_list(l4, n4)
        load_list(l5, n5)

        picked_w = [keep.tile([P, S], U32, name="picked_w%d" % i, align_bytes=64) for i in range(2)]
        picked_s = [keep.tile([P, S], U8, name="picked_s%d" % i, align_bytes=64) for i in range(2)]
        nc.vector.tensor_copy(out=picked_s[0][:], in_=xs[:].indirect(l_offs[:]))
        nc.vector.tensor_copy(out=picked_s[1][:], in_=xs[:].indirect(l_two[:]))

        grouped = {}
        w_codes = [keep.tile([P, H], U32, name="w_codes%d" % i, align_bytes=64) for i in range(3)]
        w_scales = [keep.tile([P, H], U8, name="w_scales%d" % i, align_bytes=64) for i in range(3)]

        def new_grouped(i, tag):
            grouped[i] = keep.tile([P, PACK * H], BF16, name="grouped%d" % i, tag=tag, align_bytes=64)

        def group_views(i, m0, m1):
            dst = grouped[i][:].rearrange("p (t m j) -> p m j t", t=PACK, j=PACK)[:, m0:m1]
            src = raw[i][:].rearrange("p j (m t) -> p m j t", t=PACK)[:, m0:m1]
            return dst, src

        def group_on_vector(i, m0, m1):
            dst, src = group_views(i, m0, m1)
            nc.vector.tensor_copy(out=dst, in_=src)

        def group_on_gpsimd(i, t):
            dst = grouped[i][:].rearrange("p (t a b j) -> p t a b j", t=PACK, b=8, j=PACK)[:, t]
            src = raw[i][:].rearrange("p j (a t b) -> p t a b j", t=PACK, b=8)[:, t]
            nc.gpsimd.tensor_copy(out=dst, in_=src)

        def quantize_weight(i, c0, c1):
            nc.vector.quantize_mx(
                out=w_codes[i][:, c0:c1].bitcast(FP8X4),
                scales=w_scales[i][:, c0:c1],
                in_=grouped[i][:, PACK * c0 : PACK * c1],
            )

        def product(acc, i, t, codes, scales):
            nc.tensor.matmul_mx(
                out=acc,
                lhsT=w_codes[i][:, t * P : (t + 1) * P].bitcast(FP8X4),
                lhsT_scale=w_scales[i][:, t * P : (t + 1) * P],
                rhs=codes.bitcast(FP8X4),
                rhs_scale=scales,
                start=True,
                stop=True,
            )

        nc.scalar.activation(out=half_gain[:], in_=gain[:], func=COPY, scale=0.5)
        new_grouped(0, "grouped")
        group_on_vector(0, 0, P)
        quantize_weight(0, 0, H)
        nc.vector.tensor_copy(out=picked_w[0][:], in_=xw[:].indirect(l_offs[:]))
        nc.vector.tensor_copy(out=picked_w[1][:], in_=xw[:].indirect(l_two[:]))
        y_acc = [psum.tile([P, S], F32, name="y_acc%d" % t, tag="bank%d" % t) for t in range(PACK)]
        for t in range(PACK):
            product(y_acc[t][:], 0, t, picked_w[0][:], picked_s[0][:])

        whole = slice(0, S)
        last = PACK - 1
        fetched = {}
        diffs = {}
        near = keep.tile([P, PACK, S], F32, name="near")
        far = keep.tile([P, PACK, S], F32, name="far")
        z = [keep.tile([P, PACK * HALF], BF16, name="z%d" % h, align_bytes=64) for h in range(2)]
        z_codes = [keep.tile([P, HALF], U32, name="z_codes%d" % h, align_bytes=64) for h in range(2)]
        z_scales = [keep.tile([P, HALF], U8, name="z_scales%d" % h, align_bytes=64) for h in range(2)]

        def entries(tile, c):
            return tile[:, c.start // 16 : c.stop // 16]

        def fetch(t, c, slot, with_e=False):
            n = c.stop - c.start
            fetched[t, c.start] = keep.tile([P, 3 if with_e else 2, n], F32, name="fetched%d_%d" % (t, c.start), tag=slot)
            for i, offsets in enumerate((l1, l2)):
                for c0 in range(0, n, HALF):
                    nc.scalar.activation(
                        out=fetched[t, c.start][:, i, c0 : c0 + HALF],
                        in_=y[t][:].indirect(entries(offsets, slice(c.start + c0, c.start + c0 + HALF))),
                        func=COPY,
                    )
            if with_e:
                nc.scalar.activation(out=fetched[t, c.start][:, 2, :], in_=e[t][:].indirect(entries(l3, c)), func=COPY)

        def subtract_y(t, c):
            nc.vector.tensor_tensor(
                out=diffs[t][:, :, c],
                in0=fetched[t, c.start][:, 0:2, :],
                in1=y_acc[t][:, c].unsqueeze(1).to_broadcast([P, 2, c.stop - c.start]),
                op=ALU.subtract,
            )

        def near_term(t, c):
            nc.vector.scalar_tensor_tensor(
                out=near[:, t, c], in0=diffs[t][:, 0, c], scalar=gain[:, t : t + 1], in1=d_acc[t][:, c], op0=ALU.mult, op1=ALU.mult
            )

        def far_term(t, c):
            for c0 in range(c.start, c.stop, HALF):
                nc.vector.tensor_tensor(
                    out=far[:, t, c0 : c0 + HALF],
                    in0=e[t][:].indirect(entries(l3, slice(c0, c0 + HALF))),
                    in1=diffs[t][:, 1, c0 : c0 + HALF],
                    op=ALU.mult,
                )

        def far_term_fetched(t, c):
            nc.vector.tensor_tensor(
                out=far[:, t, c], in0=fetched[t, c.start][:, 2, :], in1=diffs[t][:, 1, c], op=ALU.mult
            )

        def add_terms(h):
            nc.vector.tensor_tensor(
                out=z[h][:].rearrange("p (c i t) -> p c t i", i=4, t=PACK),
                in0=near[:, :, cols(h)].rearrange("p t (c i) -> p c t i", i=4),
                in1=far[:, :, cols(h)].rearrange("p t (c i) -> p c t i", i=4),
                op=ALU.add,
            )

        def quantize_z(h):
            nc.vector.quantize_mx(out=z_codes[h][:].bitcast(FP8X4), scales=z_scales[h][:], in_=z[h][:])

        y = {0: keep.tile([P, S], F32, name="y0")}
        e = [keep.tile([P, S], F32, name="e%d" % t) for t in range(PACK)]

        def y_on_scalar(t):
            nc.scalar.activation(out=y[t][:, whole], in_=y_acc[t][:], func=COPY)

        def d_on_scalar(t):
            nc.scalar.activation(out=e[t][:, whole], in_=d_acc[t][:], func=COPY, scale=half_gain[:, t : t + 1])

        def y_on_vector(t):
            nc.vector.tensor_copy(out=y[t][:, whole], in_=y_acc[t][:])

        first, second = cols(0), cols(1)
        y_on_scalar(0)
        fetch(0, first, "slot_a")
        fetch(0, second, "slot_b")
        new_grouped(1, "grouped")
        group_on_vector(1, 0, P)
        y[1] = shared.tile([P, S], F32, name="y1", offset=2 * S * 4)
        y[2] = shared.tile([P, S], F32, name="y2", offset=0)
        y_on_vector(1)
        quantize_weight(1, 0, P)
        quantize_weight(1, P, H)
        d_acc = [psum.tile([P, S], F32, name="d_acc%d" % t, tag="bank%d" % (PACK + t)) for t in range(PACK)]
        for t in range(PACK):
            product(d_acc[t][:], 1, t, picked_w[1][:], picked_s[1][:])
        diffs[0] = keep.tile([P, 2, S], F32, name="diffs0", tag="grouped", align_bytes=64)
        for t in range(1, PACK):
            diffs[t] = keep.tile([P, 2, S], F32, name="diffs%d" % t)
        fetch(1, first, "slot_c")
        fetch(1, second, "slot_d")
        grouped[2] = keep.tile([P, PACK * H], BF16, name="grouped2", align_bytes=64)
        for t in range(PACK):
            group_on_gpsimd(2, t)
        y_on_vector(2)
        nc.vector.tensor_scalar(out=e[0][:, whole], in0=d_acc[0][:], scalar1=half_gain[:, 0:1], scalar2=None, op0=ALU.mult)
        subtract_y(0, first)
        subtract_y(0, second)
        near_term(0, first)
        near_term(0, second)
        subtract_y(1, first)
        far_term(0, first)
        far_term(0, second)
        d_on_scalar(1)
        fetch(2, first, "slot_b")
        subtract_y(1, second)
        near_term(1, first)
        far_term(1, first)
        far_term(1, second)
        y[3] = keep.tile([P, S], F32, name="y3", tag="slot_a")
        y_on_scalar(3)
        d_on_scalar(2)
        d_on_scalar(3)
        fetch(3, first, "slot_c", True)
        subtract_y(2, first)
        near_term(1, second)
        far_term(2, first)
        subtract_y(3, first)
        near_term(2, first)
        fetch(2, second, "slot_b", True)
        far_term_fetched(3, first)
        near_term(3, first)
        quantize_weight(2, 0, H)
        add_terms(0)
        subtract_y(2, second)
        quantize_z(0)
        h_banks = ((0, 1, PACK, PACK + 1), (2, 3, PACK + 2, PACK + 3))
        h_acc = [[psum.tile([P, HALF], F32, name="h_acc0_%d" % t, tag="bank%d" % h_banks[0][t]) for t in range(PACK)]]
        for t in range(PACK):
            product(h_acc[0][t][:], 2, t, z_codes[0][:], z_scales[0][:])
        fetch(3, second, "slot_c", True)
        far_term_fetched(2, second)
        subtract_y(last, second)
        near_term(2, second)
        near_term(last, second)
        far_term_fetched(last, second)
        add_terms(1)
        wide = [diffs[t][:].rearrange("p a n -> p (a n)") for t in range(2)]
        hh = [y[0][:], wide[0], wide[1], e[0][:]]
        for t in range(PACK):
            nc.scalar.activation(out=hh[t][:, first], in_=h_acc[0][t][:], func=COPY)
        quantize_z(1)
        h_acc.append([psum.tile([P, HALF], F32, name="h_acc1_%d" % t, tag="bank%d" % h_banks[1][t]) for t in range(PACK)])
        for t in range(PACK):
            product(h_acc[1][t][:], 2, t, z_codes[1][:], z_scales[1][:])
        nc.scalar.activation(out=hh[0][:, second], in_=h_acc[1][0][:], func=COPY)
        for t in range(1, PACK):
            nc.vector.tensor_copy(out=hh[t][:, second], in_=h_acc[1][t][:])

        out_rows = out.rearrange("(a t b) j -> t a b j", t=PACK, b=8)
        at5 = [keep.tile([P, S], F32, name="at5_%d" % t) for t in range(PACK)]
        at4 = keep.tile([P, S], F32, name="at4")
        gap = {}

        def new_gap(t, c, slot):
            gap[t, c.start] = keep.tile([P, c.stop - c.start], F32, name="gap%d_%d" % (t, c.start), tag=slot)

        res = [keep.tile([P, S], F32, name="res%d" % t) for t in range(PACK)]

        def fetch5(t, c):
            nc.scalar.activation(out=at5[t][:, c], in_=hh[t].indirect(entries(l5, c)), func=COPY)

        def fused_gap(t, c, slot):
            new_gap(t, c, slot)
            nc.vector.tensor_tensor(out=gap[t, c.start][:], in0=hh[t].indirect(entries(l4, c)), in1=at5[t][:, c], op=ALU.subtract)

        def plain_gap(t, c, slot):
            new_gap(t, c, slot)
            nc.scalar.activation(out=at4[:, c], in_=hh[t].indirect(entries(l4, c)), func=COPY)
            nc.vector.tensor_tensor(out=gap[t, c.start][:], in0=at4[:, c], in1=at5[t][:, c], op=ALU.subtract)

        def finish(t, c):
            nc.vector.tensor_tensor(out=res[t][:, c], in0=gap[t, c.start][:], in1=hh[t][:, c], op=ALU.mult)
            nc.sync.dma_start(out=out_rows[t][:, :, c], in_=res[t][:, c])

        fetch5(0, first)
        fused_gap(0, first, "gap_a")
        fetch5(0, second)
        fused_gap(0, second, "gap_b")
        fetch5(1, whole)
        finish(0, first)
        finish(0, second)
        fused_gap(1, whole, "gap_a")
        fetch5(2, whole)
        fused_gap(2, whole, "gap_b")
        finish(1, whole)
        finish(2, whole)
        fetch5(last, first)
        plain_gap(last, first, "gap_a")
        fetch5(last, second)
        plain_gap(last, second, "gap_b")
        finish(last, first)
        finish(last, second)
